import numpy as np, ml_dtypes
CORES = [52,68,84,180,196,212,308,324,340]
N = 9
S, B = 3, 128
def setup_inputs(rng):
    a = (rng.standard_normal((128, 128), dtype=np.float32) / 12).astype(ml_dtypes.bfloat16)
    return {"x": rng.standard_normal((N, 128, S * B), dtype=np.float32).astype(ml_dtypes.bfloat16), "a": np.broadcast_to(a, (N, 128, 128)).copy(), "at": np.broadcast_to(a.T, (N, 128, 128)).copy()}
def setup_inputs_big(rng):
    d = setup_inputs(rng)
    for k in ("x",): d[k] = (d[k].astype(np.float32) * 1048576.0).astype(d[k].dtype)
    return d
def setup_inputs_small(rng):
    d = setup_inputs(rng)
    for k in ("x",): d[k] = (d[k].astype(np.float32) * (1 / 1048576.0)).astype(d[k].dtype)
    return d
def setup_inputs_apart(rng):
    d = setup_inputs(rng)
    f = (10.0 ** rng.permutation(np.linspace(-1.5, 1.5, N))).astype(np.float32).reshape(N, 1, 1)
    for k in ("x",): d[k] = (d[k].astype(np.float32) * f).astype(d[k].dtype)
    return d
def reference(x, a, at):
    X, A = x.astype(np.float64), a.astype(np.float64)
    y = np.zeros((N, 128, S * B)); h = np.zeros((128, B))
    for r in range(N):
        for s in range(S):
            h = A[r].T @ h + X[r][:, B * s:B * s + B]
            y[r][:, B * s:B * s + B] = h
    return {"y": y.astype(ml_dtypes.bfloat16)}

@@ -1,0 +1,193 @@
+from concourse.bass import DstId, RemoteDMATransfer
+from concourse.mybir import AluOpType
+
+S, B = 3, 128
+W_SLOTS = 11
+LAND_SLOTS = 6
+N_EVENTS = 24
+N_BANKS = 8
+
+SCRATCH = {
+    "xb": ("sbuf", [128, S * B], "bfloat16"),
+    "w": ("sbuf", [128, W_SLOTS * B], "bfloat16"),
+    "land": ("sbuf", [128, LAND_SLOTS * B], "bfloat16"),
+    "base": ("sbuf", [128, S * B], "float32"),
+    "hc": ("sbuf", [128, 2 * B], "bfloat16"),
+    "yb": ("sbuf", [128, S * B], "bfloat16"),
+}
+for _i in range(N_BANKS):
+    SCRATCH["ps%d" % _i] = ("psum", [128, 512], "float32")
+
+SEMAPHORES = (["ldx", "lda", "ldt", "sent", "stored", "arrh"] + ["arr%d" % _j for _j in range(8)]
+              + ["e%d" % _i for _i in range(N_EVENTS)])
+
+
+def rank_program(g, core, T, topo):
+    r = T.rank_of(core)
+    if r is None:
+        return
+    cores = T.cores
+    pe, ve, sy, sc = g.tensor, g.vector, g.sync, g.scalar
+
+    segs = []
+    for q, c in enumerate(cores):
+        if segs and topo.host(cores[segs[-1][-1]]) == topo.host(c):
+            segs[-1].append(q)
+        else:
+            segs.append([q])
+    head, mid, tail = segs
+    seg = [sg for sg in segs if r in sg][0]
+    p = seg.index(r)
+    last = mid[-1]
+
+    seen, n_ev, n_bank, bank_free, sent = {}, [0], [0], {}, [0]
+
+    def need(q, qn, ev):
+        if seen.get((qn, ev[0]), 0) < ev[1]:
+            q.wait_ge(T.sem[ev[0]], ev[1])
+            seen[(qn, ev[0])] = ev[1]
+
+    def new_ev():
+        n_ev[0] += 1
+        return "e%d" % (n_ev[0] - 1)
+
+    def new_bank():
+        b = n_bank[0] % N_BANKS
+        n_bank[0] += 1
+        if b in bank_free:
+            need(pe, "pe", bank_free[b])
+        return b
+
+    def mms(groups):
+        b, name, n = new_bank(), new_ev(), 0
+        for c0, terms in groups:
+            for i, (lt, rh) in enumerate(terms):
+                for ev in lt[1] + rh[1]:
+                    need(pe, "pe", ev)
+                pe.matmul(T["ps%d" % b][:, c0:c0 + B], lt[0], rh[0], i == 0, i == len(terms) - 1).then_inc(T.sem[name], 1)
+                n += 1
+        return b, (name, n)
+
+    def evac(out, width, stage, plus=None):
+        b, ev = stage
+        need(ve, "ve", ev)
+        name = new_ev()
+        if plus is None:
+            ve.tensor_copy(out, T["ps%d" % b][:, 0:width]).then_inc(T.sem[name], 1)
+        else:
+            for e in plus[1]:
+                need(ve, "ve", e)
+            ve.tensor_tensor(out, T["ps%d" % b][:, 0:width], plus[0], AluOpType.add).then_inc(T.sem[name], 1)
+        bank_free[b] = (name, 1)
+        return out, ((name, 1),)
+
+    def engines(m):
+        return bin(m).count("1")
+
+    def send(src, slot, dests, sem):
+        for ev in src[1]:
+            need(g, "g", ev)
+        m = topo.mask(core, cores[dests[0]])
+        for d in dests:
+            m &= topo.mask(core, cores[d])
+        out = T.land[:, slot * B:(slot + 1) * B]
+        ids = [topo.addr(cores[d], core) for d in dests]
+        if len(dests) == 1:
+            g.remote_dma(out_ap=out, in_ap=src[0], remote_sem=T.sem[sem], local_sem=T.sem.sent,
+                         pid=ids[0][1], routing_id=ids[0][0], dma_engine_mask=m)
+        else:
+            g.remote_dma_fused([RemoteDMATransfer(dst_ids=[DstId(rid=a, pnc=b) for a, b in ids], dma_engine_mask=m,
+                                                  remote_sem=T.sem[sem], srcs=[src[0]], dsts=[out] * len(dests),
+                                                  alu_op=0)], local_sem=T.sem.sent)
+        sent[0] += engines(m)
+
+    def slot_of(j):
+        return tail.index(j) if j in tail else j
+
+    def landed(j):
+        return (T.land[:, slot_of(j) * B:(slot_of(j) + 1) * B], (("arr%d" % j, engines(topo.mask(cores[j], core))),))
+
+    sy.dma_start(T.xb[:, :], T.x[:, :]).then_inc(T.sem.ldx, 16)
+    sc.dma_start(T.w[:, 0:B], T.a[:, :]).then_inc(T.sem.lda, 16)
+    if r > 0:
+        sc.dma_start(T.w[:, B:2 * B], T.at[:, :]).then_inc(T.sem.ldt, 16)
+    pw = {("P", 1): (T.w[:, 0:B], (("lda", 16),)), ("Q", 1): (T.w[:, B:2 * B], (("ldt", 16),))}
+
+    lv = [(T.xb[:, 0:B], (("ldx", 16),))]
+    for s in range(1, S):
+        xs = (T.xb[:, s * B:(s + 1) * B], (("ldx", 16),))
+        lv.append(evac(xs[0], B, mms([(0, [(pw[("P", 1)], lv[s - 1])])]), plus=xs))
+    l_all = (T.xb[:, :], lv[0][1] + lv[1][1] + lv[2][1])
+
+    if seg is head:
+        send(lv[2], slot_of(r), [mid[(p + i) % len(mid)] for i in range(len(mid))], "arr%d" % r)
+        if seg[p + 1:]:
+            send(lv[2], slot_of(r), seg[p + 1:], "arr%d" % r)
+    elif seg is mid:
+        send(lv[2], slot_of(r), [mid[(p + i) % len(mid)] for i in range(1, len(mid))], "arr%d" % r)
+    elif seg[p + 1:]:
+        send(lv[2], slot_of(r), seg[p + 1:], "arr%d" % r)
+
+    def P(k):
+        return pw[("P", k)]
+
+    if seg is mid:
+        levels = [[("P", 2, ("Q", 1), ("P", 1))],
+                  [("P", 3, ("Q", 1), ("P", 2)), ("Q", 3, ("P", 2), ("Q", 1))],
+                  [("P", 6, ("Q", 3), ("P", 3)), ("Q", 6, ("P", 3), ("Q", 3))],
+                  [("P", 9, ("Q", 6), ("P", 3)), ("P", 12, ("Q", 6), ("P", 6))],
+                  [("P", 15, ("Q", 6), ("P", 9))]]
+    else:
+        top = S * p if seg is head else S * (p + 1)
+        levels = []
+        if top >= 3:
+            levels = [[("P", 2, ("Q", 1), ("P", 1))], [("P", 3, ("Q", 1), ("P", 2))]]
+        if top > 3:
+            levels[1].append(("Q", 3, ("P", 2), ("Q", 1)))
+        for k0 in range(4, top + 1, 3):
+            levels.append([("P", k, ("Q", 3), ("P", k - 3)) for k in range(k0, k0 + 3)])
+    slot = 2
+    for lev in levels:
+        st = mms([(i * B, [(pw[lt], pw[rh])]) for i, (_, _, lt, rh) in enumerate(lev)])
+        _, evs = evac(T.w[:, slot * B:(slot + len(lev)) * B], len(lev) * B, st)
+        for i, (kind, k, _, _) in enumerate(lev):
+            pw[(kind, k)] = (T.w[:, (slot + i) * B:(slot + i + 1) * B], evs)
+        slot += len(lev)
+
+    def src(j):
+        return lv[2] if j == r else landed(j)
+
+    if seg is head:
+        if p == 0:
+            y = l_all
+        else:
+            st = mms([(s * B, [(P(S * (r - 1 - j) + s + 1), src(j)) for j in range(r - 1, -1, -1)]) for s in range(S)])
+            y = evac(T.yb[:, :], S * B, st, plus=l_all)
+    elif seg is mid:
+        order = ([r] + sorted([j for j in mid if j != r], key=lambda j: (p - mid.index(j) - 1) % len(mid))
+                 + sorted(head, key=lambda j: (p - head.index(j)) % len(mid)))
+        st = mms([(0, [(P(S * (last - j)), src(j)) for j in order if j != last])])
+        carry = evac(T.hc[:, 0:B], B, st, plus=src(last))
+        partner = [q for q in tail if topo.chip(cores[q]) == topo.chip(core)][0]
+        send(carry, len(tail) - 1, [partner], "arrh")
+        st = mms([(0, [(P(S * (r - 1 - j)), src(j)) for j in range(r - 2, -1, -1)])])
+        hp = evac(T.hc[:, B:2 * B], B, st, plus=src(r - 1))
+        st = mms([(s * B, [(P(s + 1), hp)]) for s in range(S)])
+        y = evac(T.yb[:, :], S * B, st, plus=l_all)
+    else:
+        base = l_all
+        if p > 0:
+            st = mms([(s * B, [(P(S * (r - 1 - j) + s + 1), src(j)) for j in seg[:p]]) for s in range(S)])
+            base = evac(T.base[:, :], S * B, st, plus=l_all)
+        giver = [q for q in mid if topo.chip(cores[q]) == topo.chip(core)][0]
+        hs = len(tail) - 1
+        carry = (T.land[:, hs * B:(hs + 1) * B], (("arrh", engines(topo.mask(cores[giver], core))),))
+        st = mms([(s * B, [(P(S * p + s + 1), carry)]) for s in range(S)])
+        y = evac(T.yb[:, :], S * B, st, plus=base)
+
+    for ev in y[1]:
+        need(sy, "sy", ev)
+    sy.dma_start(T.y[:, :], y[0]).then_inc(T.sem.stored, 16)
+    sy.wait_ge(T.sem.stored, 16)
+    if sent[0]:
+        g.wait_ge(T.sem.sent, sent[0])

@@ -2,15 +2,19 @@ from concourse.bass import DstId, RemoteDMATransfer
 from concourse.mybir import AluOpType
 
 S, B = 3, 128
+HB = B // 2
 W_SLOTS = 11
 LAND_SLOTS = 6
-N_EVENTS = 24
+N_EVENTS = 56
 N_BANKS = 8
 
 SCRATCH = {
     "xb": ("sbuf", [128, S * B], "bfloat16"),
+    "l2b": ("sbuf", [128, B], "bfloat16"),
+    "m1b": ("sbuf", [128, B], "bfloat16"),
     "w": ("sbuf", [128, W_SLOTS * B], "bfloat16"),
     "land": ("sbuf", [128, LAND_SLOTS * B], "bfloat16"),
+    "lx": ("sbuf", [128, B], "bfloat16"),
     "base": ("sbuf", [128, S * B], "float32"),
     "hc": ("sbuf", [128, 2 * B], "bfloat16"),
     "yb": ("sbuf", [128, S * B], "bfloat16"),
@@ -18,7 +22,7 @@ SCRATCH = {
 for _i in range(N_BANKS):
     SCRATCH["ps%d" % _i] = ("psum", [128, 512], "float32")
 
-SEMAPHORES = (["ldx", "lda", "ldt", "sent", "stored", "arrh"] + ["arr%d" % _j for _j in range(8)]
+SEMAPHORES = (["ldx", "lda", "ldt", "sent", "st0", "st1", "arrh", "arx"] + ["arr%d" % _j for _j in range(8)]
               + ["e%d" % _i for _i in range(N_EVENTS)])
 
 
@@ -38,6 +42,7 @@ def rank_program(g, core, T, topo):
     head, mid, tail = segs
     seg = [sg for sg in segs if r in sg][0]
     p = seg.index(r)
+    nm = len(mid)
     last = mid[-1]
 
     seen, n_ev, n_bank, bank_free, sent = {}, [0], [0], {}, [0]
@@ -51,25 +56,21 @@ def rank_program(g, core, T, topo):
         n_ev[0] += 1
         return "e%d" % (n_ev[0] - 1)
 
-    def new_bank():
+    def mms(width, terms):
         b = n_bank[0] % N_BANKS
         n_bank[0] += 1
-        if b in bank_free:
-            need(pe, "pe", bank_free[b])
-        return b
+        for ev in bank_free.get(b, []):
+            need(pe, "pe", ev)
+        bank_free[b] = []
+        name = new_ev()
+        for i, (lt, rh) in enumerate(terms):
+            for ev in lt[1] + rh[1]:
+                need(pe, "pe", ev)
+            pe.matmul(T["ps%d" % b][:, 0:width], lt[0], rh[0], i == 0, i == len(terms) - 1).then_inc(T.sem[name], 1)
+        return b, (name, len(terms)), width
 
-    def mms(groups):
-        b, name, n = new_bank(), new_ev(), 0
-        for c0, terms in groups:
-            for i, (lt, rh) in enumerate(terms):
-                for ev in lt[1] + rh[1]:
-                    need(pe, "pe", ev)
-                pe.matmul(T["ps%d" % b][:, c0:c0 + B], lt[0], rh[0], i == 0, i == len(terms) - 1).then_inc(T.sem[name], 1)
-                n += 1
-        return b, (name, n)
-
-    def evac(out, width, stage, plus=None):
-        b, ev = stage
+    def evac(out, stage, plus=None):
+        b, ev, width = stage
         need(ve, "ve", ev)
         name = new_ev()
         if plus is None:
@@ -78,19 +79,18 @@ def rank_program(g, core, T, topo):
             for e in plus[1]:
                 need(ve, "ve", e)
             ve.tensor_tensor(out, T["ps%d" % b][:, 0:width], plus[0], AluOpType.add).then_inc(T.sem[name], 1)
-        bank_free[b] = (name, 1)
+        bank_free[b].append((name, 1))
         return out, ((name, 1),)
 
     def engines(m):
         return bin(m).count("1")
 
-    def send(src, slot, dests, sem):
+    def send(src, out, dests, sem):
         for ev in src[1]:
             need(g, "g", ev)
         m = topo.mask(core, cores[dests[0]])
         for d in dests:
             m &= topo.mask(core, cores[d])
-        out = T.land[:, slot * B:(slot + 1) * B]
         ids = [topo.addr(cores[d], core) for d in dests]
         if len(dests) == 1:
             g.remote_dma(out_ap=out, in_ap=src[0], remote_sem=T.sem[sem], local_sem=T.sem.sent,
@@ -101,93 +101,121 @@ def rank_program(g, core, T, topo):
                                                   alu_op=0)], local_sem=T.sem.sent)
         sent[0] += engines(m)
 
-    def slot_of(j):
-        return tail.index(j) if j in tail else j
+    def slot(j):
+        k = tail.index(j) if j in tail else j
+        return T.land[:, k * B:(k + 1) * B]
 
     def landed(j):
-        return (T.land[:, slot_of(j) * B:(slot_of(j) + 1) * B], (("arr%d" % j, engines(topo.mask(cores[j], core))),))
+        return slot(j), (("arr%d" % j, engines(topo.mask(cores[j], core))),)
+
+    def cols(buf, c0, h):
+        return buf[:, c0 + h * HB:c0 + (h + 1) * HB]
 
     sy.dma_start(T.xb[:, :], T.x[:, :]).then_inc(T.sem.ldx, 16)
     sc.dma_start(T.w[:, 0:B], T.a[:, :]).then_inc(T.sem.lda, 16)
     if r > 0:
         sc.dma_start(T.w[:, B:2 * B], T.at[:, :]).then_inc(T.sem.ldt, 16)
+    LDX = (("ldx", 16),)
     pw = {("P", 1): (T.w[:, 0:B], (("lda", 16),)), ("Q", 1): (T.w[:, B:2 * B], (("ldt", 16),))}
 
-    lv = [(T.xb[:, 0:B], (("ldx", 16),))]
-    for s in range(1, S):
-        xs = (T.xb[:, s * B:(s + 1) * B], (("ldx", 16),))
-        lv.append(evac(xs[0], B, mms([(0, [(pw[("P", 1)], lv[s - 1])])]), plus=xs))
-    l_all = (T.xb[:, :], lv[0][1] + lv[1][1] + lv[2][1])
-
     if seg is head:
-        send(lv[2], slot_of(r), [mid[(p + i) % len(mid)] for i in range(len(mid))], "arr%d" % r)
-        if seg[p + 1:]:
-            send(lv[2], slot_of(r), seg[p + 1:], "arr%d" % r)
-    elif seg is mid:
-        send(lv[2], slot_of(r), [mid[(p + i) % len(mid)] for i in range(1, len(mid))], "arr%d" % r)
-    elif seg[p + 1:]:
-        send(lv[2], slot_of(r), seg[p + 1:], "arr%d" % r)
+        send((T.xb[:, 2 * B:3 * B], LDX), T.lx[:, :], [mid[(p + 2) % nm]], "arx")
+
+    if seg is mid:
+        steps = [("P", 2, ("Q", 1), ("P", 1)),
+                 ("P", 3, ("Q", 1), ("P", 2)), ("Q", 3, ("P", 2), ("Q", 1)),
+                 ("Q", 6, ("P", 3), ("Q", 3)), ("P", 6, ("Q", 3), ("P", 3)),
+                 ("P", 9, ("Q", 6), ("P", 3)), ("P", 12, ("Q", 6), ("P", 6)),
+                 ("P", 15, ("Q", 6), ("P", 9))]
+    else:
+        top = S * p if seg is head else S * (p + 1)
+        steps = []
+        if top >= 3:
+            steps = [("P", 2, ("Q", 1), ("P", 1)), ("P", 3, ("Q", 1), ("P", 2))]
+        if top > 3:
+            steps.append(("Q", 3, ("P", 2), ("Q", 1)))
+        steps += [("P", k, ("Q", 3), ("P", k - 3)) for k in range(4, top + 1)]
+    n_slot = [2]
+
+    def power(step):
+        kind, k, lt, rh = step
+        out = T.w[:, n_slot[0] * B:(n_slot[0] + 1) * B]
+        n_slot[0] += 1
+        pw[(kind, k)] = evac(out, mms(B, [(pw[lt], pw[rh])]))
 
     def P(k):
         return pw[("P", k)]
 
+    st = [mms(HB, [(P(1), (cols(T.xb, 0, h), LDX))]) for h in range(2)]
+    l1h = [evac(cols(T.xb, B, h), st[h], plus=(cols(T.xb, B, h), LDX)) for h in range(2)]
     if seg is mid:
-        levels = [[("P", 2, ("Q", 1), ("P", 1))],
-                  [("P", 3, ("Q", 1), ("P", 2)), ("Q", 3, ("P", 2), ("Q", 1))],
-                  [("P", 6, ("Q", 3), ("P", 3)), ("Q", 6, ("P", 3), ("Q", 3))],
-                  [("P", 9, ("Q", 6), ("P", 3)), ("P", 12, ("Q", 6), ("P", 6))],
-                  [("P", 15, ("Q", 6), ("P", 9))]]
-    else:
-        top = S * p if seg is head else S * (p + 1)
-        levels = []
-        if top >= 3:
-            levels = [[("P", 2, ("Q", 1), ("P", 1))], [("P", 3, ("Q", 1), ("P", 2))]]
-        if top > 3:
-            levels[1].append(("Q", 3, ("P", 2), ("Q", 1)))
-        for k0 in range(4, top + 1, 3):
-            levels.append([("P", k, ("Q", 3), ("P", k - 3)) for k in range(k0, k0 + 3)])
-    slot = 2
-    for lev in levels:
-        st = mms([(i * B, [(pw[lt], pw[rh])]) for i, (_, _, lt, rh) in enumerate(lev)])
-        _, evs = evac(T.w[:, slot * B:(slot + len(lev)) * B], len(lev) * B, st)
-        for i, (kind, k, _, _) in enumerate(lev):
-            pw[(kind, k)] = (T.w[:, (slot + i) * B:(slot + i + 1) * B], evs)
-        slot += len(lev)
+        power(steps.pop(0))
+    st = [mms(HB, [(P(1), l1h[h])]) for h in range(2)]
+    l2h = [evac(cols(T.l2b, 0, h), st[h], plus=(cols(T.xb, 2 * B, h), LDX)) for h in range(2)]
+    lv = [(T.xb[:, 0:B], LDX), (T.xb[:, B:2 * B], l1h[0][1] + l1h[1][1]), (T.l2b[:, :], l2h[0][1] + l2h[1][1])]
 
-    def src(j):
-        return lv[2] if j == r else landed(j)
+    if seg is head:
+        m1h = [evac(cols(T.m1b, 0, h), st[h]) for h in range(2)]
+        send(lv[2], slot(r), [mid[p % nm], mid[(p + 1) % nm]], "arr%d" % r)
+        send((T.m1b[:, :], m1h[0][1] + m1h[1][1]), slot(r), [mid[(p + 2) % nm]], "arr%d" % r)
+        if seg[p + 1:]:
+            send(lv[2], slot(r), seg[p + 1:], "arr%d" % r)
+    elif seg is mid:
+        send(lv[2], slot(r), [mid[(p + i) % nm] for i in range(1, nm)], "arr%d" % r)
+    elif seg[p + 1:]:
+        send(lv[2], slot(r), seg[p + 1:], "arr%d" % r)
+
+    for step in steps:
+        power(step)
+
+    split = head[(p + 1) % nm] if seg is mid else None
+
+    def parts(j):
+        if j == r:
+            return [lv[2]]
+        if j == split:
+            return [(T.lx[:, :], (("arx", engines(topo.mask(cores[j], core))),)), landed(j)]
+        return [landed(j)]
+
+    def finish(terms, plus):
+        sts = [mms(B, terms[s]) for s in range(S)]
+        ys = [evac(T.yb[:, s * B:(s + 1) * B], sts[s], plus=plus[s]) for s in range(S)]
+        return [((T.yb[:, 0:B], ys[0][1]), 0, B), ((T.yb[:, B:S * B], ys[1][1] + ys[2][1]), B, S * B)]
 
     if seg is head:
         if p == 0:
-            y = l_all
+            stores = [((T.xb[:, 0:2 * B], lv[0][1] + lv[1][1]), 0, 2 * B), (lv[2], 2 * B, S * B)]
         else:
-            st = mms([(s * B, [(P(S * (r - 1 - j) + s + 1), src(j)) for j in range(r - 1, -1, -1)]) for s in range(S)])
-            y = evac(T.yb[:, :], S * B, st, plus=l_all)
+            stores = finish([[(P(S * (r - 1 - j) + s + 1), v) for j in range(r - 1, -1, -1) for v in parts(j)]
+                             for s in range(S)], lv)
     elif seg is mid:
-        order = ([r] + sorted([j for j in mid if j != r], key=lambda j: (p - mid.index(j) - 1) % len(mid))
-                 + sorted(head, key=lambda j: (p - head.index(j)) % len(mid)))
-        st = mms([(0, [(P(S * (last - j)), src(j)) for j in order if j != last])])
-        carry = evac(T.hc[:, 0:B], B, st, plus=src(last))
+        due = [(r, lv[2]), (split, parts(split)[0])]
+        due += [(j, landed(j)) for j in sorted([j for j in mid if j != r], key=lambda j: (p - mid.index(j) - 1) % nm)]
+        due += [(head[p % nm], landed(head[p % nm])), (head[(p + 2) % nm], landed(head[(p + 2) % nm])),
+                (split, parts(split)[1])]
+        due = [(S * (last - j), v) for j, v in due if j != last]
+        high = max(k for k, _ in due)
+        due = [t for t in due[:-1] if t[0] != high] + [t for t in due[:-1] if t[0] == high] + due[-1:]
+        carry = evac(T.hc[:, 0:B], mms(B, [(P(k), v) for k, v in due]), plus=parts(last)[0])
         partner = [q for q in tail if topo.chip(cores[q]) == topo.chip(core)][0]
-        send(carry, len(tail) - 1, [partner], "arrh")
-        st = mms([(0, [(P(S * (r - 1 - j)), src(j)) for j in range(r - 2, -1, -1)])])
-        hp = evac(T.hc[:, B:2 * B], B, st, plus=src(r - 1))
-        st = mms([(s * B, [(P(s + 1), hp)]) for s in range(S)])
-        y = evac(T.yb[:, :], S * B, st, plus=l_all)
+        send(carry, T.land[:, (len(tail) - 1) * B:len(tail) * B], [partner], "arrh")
+        assert r - 1 != split
+        hp = evac(T.hc[:, B:2 * B], mms(B, [(P(S * (r - 1 - j)), v) for j in range(r - 2, -1, -1) for v in parts(j)]),
+                  plus=parts(r - 1)[0])
+        stores = finish([[(P(s + 1), hp)] for s in range(S)], lv)
     else:
-        base = l_all
+        base = lv
         if p > 0:
-            st = mms([(s * B, [(P(S * (r - 1 - j) + s + 1), src(j)) for j in seg[:p]]) for s in range(S)])
-            base = evac(T.base[:, :], S * B, st, plus=l_all)
+            sts = [mms(B, [(P(S * (r - 1 - j) + s + 1), landed(j)) for j in seg[:p]]) for s in range(S)]
+            base = [evac(T.base[:, s * B:(s + 1) * B], sts[s], plus=lv[s]) for s in range(S)]
         giver = [q for q in mid if topo.chip(cores[q]) == topo.chip(core)][0]
-        hs = len(tail) - 1
-        carry = (T.land[:, hs * B:(hs + 1) * B], (("arrh", engines(topo.mask(cores[giver], core))),))
-        st = mms([(s * B, [(P(S * p + s + 1), carry)]) for s in range(S)])
-        y = evac(T.yb[:, :], S * B, st, plus=base)
+        carry = (T.land[:, (len(tail) - 1) * B:len(tail) * B], (("arrh", engines(topo.mask(cores[giver], core))),))
+        stores = finish([[(P(S * p + s + 1), carry)] for s in range(S)], base)
 
-    for ev in y[1]:
-        need(sy, "sy", ev)
-    sy.dma_start(T.y[:, :], y[0]).then_inc(T.sem.stored, 16)
-    sy.wait_ge(T.sem.stored, 16)
+    for (q, qn, sem), (v, c0, c1) in zip(((sc, "sc", "st0"), (sy, "sy", "st1")), stores):
+        for ev in v[1]:
+            need(q, qn, ev)
+        q.dma_start(T.y[:, c0:c1], v[0]).then_inc(T.sem[sem], 16)
+        q.wait_ge(T.sem[sem], 16)
     if sent[0]:
         g.wait_ge(T.sem.sent, sent[0])

from concourse.bass import DstId, RemoteDMATransfer
from concourse.mybir import AluOpType

S, B = 3, 128
HB = B // 2
W_SLOTS = 11
LAND_SLOTS = 6
N_EVENTS = 56
N_BANKS = 8

SCRATCH = {
    "xb": ("sbuf", [128, S * B], "bfloat16"),
    "l2b": ("sbuf", [128, B], "bfloat16"),
    "m1b": ("sbuf", [128, B], "bfloat16"),
    "w": ("sbuf", [128, W_SLOTS * B], "bfloat16"),
    "land": ("sbuf", [128, LAND_SLOTS * B], "bfloat16"),
    "lx": ("sbuf", [128, B], "bfloat16"),
    "base": ("sbuf", [128, S * B], "float32"),
    "hc": ("sbuf", [128, 2 * B], "bfloat16"),
    "yb": ("sbuf", [128, S * B], "bfloat16"),
}
for _i in range(N_BANKS):
    SCRATCH["ps%d" % _i] = ("psum", [128, 512], "float32")

SEMAPHORES = (["ldx", "lda", "ldt", "sent", "st0", "st1", "arrh", "arx"] + ["arr%d" % _j for _j in range(8)]
              + ["e%d" % _i for _i in range(N_EVENTS)])


def rank_program(g, core, T, topo):
    r = T.rank_of(core)
    if r is None:
        return
    cores = T.cores
    pe, ve, sy, sc = g.tensor, g.vector, g.sync, g.scalar

    segs = []
    for q, c in enumerate(cores):
        if segs and topo.host(cores[segs[-1][-1]]) == topo.host(c):
            segs[-1].append(q)
        else:
            segs.append([q])
    head, mid, tail = segs
    seg = [sg for sg in segs if r in sg][0]
    p = seg.index(r)
    nm = len(mid)
    last = mid[-1]

    seen, n_ev, n_bank, bank_free, sent = {}, [0], [0], {}, [0]

    def need(q, qn, ev):
        if seen.get((qn, ev[0]), 0) < ev[1]:
            q.wait_ge(T.sem[ev[0]], ev[1])
            seen[(qn, ev[0])] = ev[1]

    def new_ev():
        n_ev[0] += 1
        return "e%d" % (n_ev[0] - 1)

    def mms(width, terms):
        b = n_bank[0] % N_BANKS
        n_bank[0] += 1
        for ev in bank_free.get(b, []):
            need(pe, "pe", ev)
        bank_free[b] = []
        name = new_ev()
        for i, (lt, rh) in enumerate(terms):
            for ev in lt[1] + rh[1]:
                need(pe, "pe", ev)
            pe.matmul(T["ps%d" % b][:, 0:width], lt[0], rh[0], i == 0, i == len(terms) - 1).then_inc(T.sem[name], 1)
        return b, (name, len(terms)), width

    def evac(out, stage, plus=None):
        b, ev, width = stage
        need(ve, "ve", ev)
        name = new_ev()
        if plus is None:
            ve.tensor_copy(out, T["ps%d" % b][:, 0:width]).then_inc(T.sem[name], 1)
        else:
            for e in plus[1]:
                need(ve, "ve", e)
            ve.tensor_tensor(out, T["ps%d" % b][:, 0:width], plus[0], AluOpType.add).then_inc(T.sem[name], 1)
        bank_free[b].append((name, 1))
        return out, ((name, 1),)

    def engines(m):
        return bin(m).count("1")

    def send(src, out, dests, sem):
        for ev in src[1]:
            need(g, "g", ev)
        m = topo.mask(core, cores[dests[0]])
        for d in dests:
            m &= topo.mask(core, cores[d])
        ids = [topo.addr(cores[d], core) for d in dests]
        if len(dests) == 1:
            g.remote_dma(out_ap=out, in_ap=src[0], remote_sem=T.sem[sem], local_sem=T.sem.sent,
                         pid=ids[0][1], routing_id=ids[0][0], dma_engine_mask=m)
        else:
            g.remote_dma_fused([RemoteDMATransfer(dst_ids=[DstId(rid=a, pnc=b) for a, b in ids], dma_engine_mask=m,
                                                  remote_sem=T.sem[sem], srcs=[src[0]], dsts=[out] * len(dests),
                                                  alu_op=0)], local_sem=T.sem.sent)
        sent[0] += engines(m)

    def slot(j):
        k = tail.index(j) if j in tail else j
        return T.land[:, k * B:(k + 1) * B]

    def landed(j):
        return slot(j), (("arr%d" % j, engines(topo.mask(cores[j], core))),)

    def cols(buf, c0, h):
        return buf[:, c0 + h * HB:c0 + (h + 1) * HB]

    sy.dma_start(T.xb[:, :], T.x[:, :]).then_inc(T.sem.ldx, 16)
    sc.dma_start(T.w[:, 0:B], T.a[:, :]).then_inc(T.sem.lda, 16)
    if r > 0:
        sc.dma_start(T.w[:, B:2 * B], T.at[:, :]).then_inc(T.sem.ldt, 16)
    LDX = (("ldx", 16),)
    pw = {("P", 1): (T.w[:, 0:B], (("lda", 16),)), ("Q", 1): (T.w[:, B:2 * B], (("ldt", 16),))}

    if seg is head:
        send((T.xb[:, 2 * B:3 * B], LDX), T.lx[:, :], [mid[(p + 2) % nm]], "arx")

    if seg is mid:
        steps = [("P", 2, ("Q", 1), ("P", 1)),
                 ("P", 3, ("Q", 1), ("P", 2)), ("Q", 3, ("P", 2), ("Q", 1)),
                 ("Q", 6, ("P", 3), ("Q", 3)), ("P", 6, ("Q", 3), ("P", 3)),
                 ("P", 9, ("Q", 6), ("P", 3)), ("P", 12, ("Q", 6), ("P", 6)),
                 ("P", 15, ("Q", 6), ("P", 9))]
    else:
        top = S * p if seg is head else S * (p + 1)
        steps = []
        if top >= 3:
            steps = [("P", 2, ("Q", 1), ("P", 1)), ("P", 3, ("Q", 1), ("P", 2))]
        if top > 3:
            steps.append(("Q", 3, ("P", 2), ("Q", 1)))
        steps += [("P", k, ("Q", 3), ("P", k - 3)) for k in range(4, top + 1)]
    n_slot = [2]

    def power(step):
        kind, k, lt, rh = step
        out = T.w[:, n_slot[0] * B:(n_slot[0] + 1) * B]
        n_slot[0] += 1
        pw[(kind, k)] = evac(out, mms(B, [(pw[lt], pw[rh])]))

    def P(k):
        return pw[("P", k)]

    st = [mms(HB, [(P(1), (cols(T.xb, 0, h), LDX))]) for h in range(2)]
    l1h = [evac(cols(T.xb, B, h), st[h], plus=(cols(T.xb, B, h), LDX)) for h in range(2)]
    if seg is mid:
        power(steps.pop(0))
    st = [mms(HB, [(P(1), l1h[h])]) for h in range(2)]
    l2h = [evac(cols(T.l2b, 0, h), st[h], plus=(cols(T.xb, 2 * B, h), LDX)) for h in range(2)]
    lv = [(T.xb[:, 0:B], LDX), (T.xb[:, B:2 * B], l1h[0][1] + l1h[1][1]), (T.l2b[:, :], l2h[0][1] + l2h[1][1])]

    if seg is head:
        m1h = [evac(cols(T.m1b, 0, h), st[h]) for h in range(2)]
        send(lv[2], slot(r), [mid[p % nm], mid[(p + 1) % nm]], "arr%d" % r)
        send((T.m1b[:, :], m1h[0][1] + m1h[1][1]), slot(r), [mid[(p + 2) % nm]], "arr%d" % r)
        if seg[p + 1:]:
            send(lv[2], slot(r), seg[p + 1:], "arr%d" % r)
    elif seg is mid:
        send(lv[2], slot(r), [mid[(p + i) % nm] for i in range(1, nm)], "arr%d" % r)
    elif seg[p + 1:]:
        send(lv[2], slot(r), seg[p + 1:], "arr%d" % r)

    for step in steps:
        power(step)

    split = head[(p + 1) % nm] if seg is mid else None

    def parts(j):
        if j == r:
            return [lv[2]]
        if j == split:
            return [(T.lx[:, :], (("arx", engines(topo.mask(cores[j], core))),)), landed(j)]
        return [landed(j)]

    def finish(terms, plus):
        sts = [mms(B, terms[s]) for s in range(S)]
        ys = [evac(T.yb[:, s * B:(s + 1) * B], sts[s], plus=plus[s]) for s in range(S)]
        return [((T.yb[:, 0:B], ys[0][1]), 0, B), ((T.yb[:, B:S * B], ys[1][1] + ys[2][1]), B, S * B)]

    if seg is head:
        if p == 0:
            stores = [((T.xb[:, 0:2 * B], lv[0][1] + lv[1][1]), 0, 2 * B), (lv[2], 2 * B, S * B)]
        else:
            stores = finish([[(P(S * (r - 1 - j) + s + 1), v) for j in range(r - 1, -1, -1) for v in parts(j)]
                             for s in range(S)], lv)
    elif seg is mid:
        due = [(r, lv[2]), (split, parts(split)[0])]
        due += [(j, landed(j)) for j in sorted([j for j in mid if j != r], key=lambda j: (p - mid.index(j) - 1) % nm)]
        due += [(head[p % nm], landed(head[p % nm])), (head[(p + 2) % nm], landed(head[(p + 2) % nm])),
                (split, parts(split)[1])]
        due = [(S * (last - j), v) for j, v in due if j != last]
        high = max(k for k, _ in due)
        due = [t for t in due[:-1] if t[0] != high] + [t for t in due[:-1] if t[0] == high] + due[-1:]
        carry = evac(T.hc[:, 0:B], mms(B, [(P(k), v) for k, v in due]), plus=parts(last)[0])
        partner = [q for q in tail if topo.chip(cores[q]) == topo.chip(core)][0]
        send(carry, T.land[:, (len(tail) - 1) * B:len(tail) * B], [partner], "arrh")
        assert r - 1 != split
        hp = evac(T.hc[:, B:2 * B], mms(B, [(P(S * (r - 1 - j)), v) for j in range(r - 2, -1, -1) for v in parts(j)]),
                  plus=parts(r - 1)[0])
        stores = finish([[(P(s + 1), hp)] for s in range(S)], lv)
    else:
        base = lv
        if p > 0:
            sts = [mms(B, [(P(S * (r - 1 - j) + s + 1), landed(j)) for j in seg[:p]]) for s in range(S)]
            base = [evac(T.base[:, s * B:(s + 1) * B], sts[s], plus=lv[s]) for s in range(S)]
        giver = [q for q in mid if topo.chip(cores[q]) == topo.chip(core)][0]
        carry = (T.land[:, (len(tail) - 1) * B:len(tail) * B], (("arrh", engines(topo.mask(cores[giver], core))),))
        stores = finish([[(P(S * p + s + 1), carry)] for s in range(S)], base)

    for (q, qn, sem), (v, c0, c1) in zip(((sc, "sc", "st0"), (sy, "sy", "st1")), stores):
        for ev in v[1]:
            need(q, qn, ev)
        q.dma_start(T.y[:, c0:c1], v[0]).then_inc(T.sem[sem], 16)
        q.wait_ge(T.sem[sem], 16)
    if sent[0]:
        g.wait_ge(T.sem.sent, sent[0])
